import numpy as np
import ml_dtypes


def mxq(x, axis, fmt="e4m3"):
    dtype, down = {"e4m3": (ml_dtypes.float8_e4m3fn, 7), "e5m2": (ml_dtypes.float8_e5m2, 14)}[fmt]
    v = np.moveaxis(np.asarray(x, np.float32).astype(ml_dtypes.bfloat16).astype(np.float64), axis, -1)
    blocks = v.reshape(v.shape[:-1] + (-1, 32))
    amax = np.abs(blocks).max(-1, keepdims=True)
    byte = np.maximum(np.where(amax > 0, np.frexp(amax)[1] - 1 + 127, 0) - down, 1)
    scale = np.exp2(byte - 127.0)
    codes = (blocks / scale).astype(np.float32).astype(dtype).astype(np.float64)
    return np.moveaxis((codes * scale).reshape(v.shape), -1, axis)


WIDE = False


def mx_kscale(k):
    if not WIDE:
        return np.ones(k)
    levels = np.array([10, -10, 5, -5, 0])
    if k % 512:
        return np.exp2(np.random.permutation(np.resize(levels, k // 32))).repeat(32)
    a = np.empty((k // 512, 16))
    for p in range(k // 512):
        a[p, :8] = np.random.permutation(np.resize(levels, 8))
        for g in range(8):
            far = levels[np.abs(levels - a[p, g]) >= 10]
            a[p, g + 8] = far[np.random.randint(len(far))]
    return np.exp2(a.ravel()).repeat(32)


def f64(x):
    return np.asarray(x).astype(np.float64)


def striped(idx):
    return np.tile(idx.reshape(-1, 16).T, (8, 1)).astype(np.uint16)


def unstriped(offs):
    return offs[:16].T.reshape(-1).astype(np.int64)


def striped8(idx):
    return np.concatenate([x.reshape(-1, 16).T for x in idx]).astype(np.uint16)


def runs(offs, k):
    lists = np.stack([offs[16 * r : 16 * r + 16].T.reshape(-1) for r in range(8)]).astype(np.int64)
    return lists[np.arange(k) % 512 // 64]


def pack_weight(w):
    k, n = w.shape
    w = f64(np.asarray(w, np.float32).astype(ml_dtypes.bfloat16)).reshape(k // 32, 32, n)
    amax = np.abs(w).max(1)
    byte = np.clip(np.where(amax > 0, np.frexp(amax)[1] - 1 + 127 - 7, 1), 1, 254)
    scaled = (w * np.exp2(127.0 - byte)[:, None, :]).reshape(k, n).astype(np.float32)
    words = np.ascontiguousarray(scaled.reshape(k // 512, 128, 4, n).transpose(0, 1, 3, 2)).astype(ml_dtypes.float8_e4m3fn).view(np.uint8)
    return words, np.ascontiguousarray(byte.astype(np.uint8).reshape(k // 512, 16, n))


def unpack_weight(words, scales):
    g, p, n, _ = words.shape
    vals = np.ascontiguousarray(words).view(ml_dtypes.float8_e4m3fn).astype(np.float64) * np.repeat(np.exp2(scales.astype(np.float64) - 127.0), 8, axis=1)[..., None]
    return vals.transpose(0, 1, 3, 2).reshape(g * 512, n)


K, T, S, N, G, H, W, U = 512, 1024, 256, 512, 2048, 512, 128, 1024


def setup_inputs():
    n = np.random.standard_normal
    s = mx_kscale(K)[:, None]
    u = mx_kscale(K)
    packed_xT = pack_weight(n((K, T)) * s)
    packed_dT = pack_weight(n((K, G)) / s)
    perm = np.random.permutation(S)
    return {
        "x_words": packed_xT[0],
        "x_scales": packed_xT[1],
        "d_words": packed_dT[0],
        "d_scales": packed_dT[1],
        "gn": (np.random.uniform(0.5, 1.5, (H, 1)) * u[:, None]).astype(np.float32),
        "w1": (n((H, N)) / np.sqrt(H) / u[:, None]).astype(np.float32),
        "offs": striped(np.random.permutation(T)[:S]),
        "ka": striped8(np.random.randint(0, G, (8, H))),
        "kb": striped8(np.random.randint(0, G, (8, H))),
        "n1": striped(perm[:W]),
        "n2": striped(perm[W:]),
        "n3": striped(np.random.permutation(S)),
        "n4": striped(np.random.permutation(U)[:S]),
        "n5": striped(np.random.permutation(S)),
    }


def reference(x_words, x_scales, d_words, d_scales, gn, w1, offs, ka, kb, n1, n2, n3, n4, n5):
    d_ka = unpack_weight(d_words, d_scales)[np.arange(K)[:, None], runs(ka, K)]
    xq = unpack_weight(x_words, x_scales)[:, unstriped(offs)]
    d_kb = unpack_weight(d_words, d_scales)[np.arange(K)[:, None], runs(kb, K)]
    h = 0.0625 * (d_ka.T @ xq + d_kb.T @ xq)
    pa = h[:, unstriped(n1)]
    pb = h[:, unstriped(n2)]
    rb = np.minimum(pa, pb)
    ra = np.maximum(pa, pb)
    ds = np.zeros((H, S))
    ds[:, unstriped(n1)] = ra
    dt = ds.copy()
    dt[:, unstriped(n2)] = rb
    z = f64(gn) * (dt - dt[:, unstriped(n3)])
    h2 = mxq(f64(w1), 0, "e4m3").T @ mxq(z, 0, "e4m3")
    nw = np.maximum(h2, h2[:, unstriped(n5)])
    out = np.zeros((N, U))
    out[:, unstriped(n4)] = nw
    return out

@@ -1,0 +1,225 @@
+from contextlib import ExitStack
+
+import concourse.mybir as mybir
+from concourse.masks import make_identity
+
+K, T, S, N, G, H, W, U = 512, 1024, 256, 512, 2048, 512, 128, 1024
+FLOPS = 2 * (2 * K * H * S) + 2 * H * N * S
+
+F32 = mybir.dt.float32
+BF16 = mybir.dt.bfloat16
+I32 = mybir.dt.int32
+U32 = mybir.dt.uint32
+U16 = mybir.dt.uint16
+U8 = mybir.dt.uint8
+FP8X4 = mybir.dt.float8_e4m3fn_x4
+ALU = mybir.AluOpType
+COPY = mybir.ActivationFunctionType.Copy
+
+P = 128
+PIECE = 256
+
+
+def tile_picked_aqlorddpags_none_p_kernel(
+    tc, x_words, x_scales, d_words, d_scales, gn, w1, offs, ka, kb, n1, n2, n3, n4, n5, out
+):
+    nc = tc.nc
+    with ExitStack() as ctx:
+        lists = ctx.enter_context(tc.tile_pool(name="lists", bufs=1))
+        keep = ctx.enter_context(tc.tile_pool(name="keep", bufs=1))
+        ps_h = ctx.enter_context(tc.psum_pool(name="ps_h", bufs=4))
+        ps_t = ctx.enter_context(tc.psum_pool(name="ps_t", bufs=2))
+        ps_w = ctx.enter_context(tc.psum_pool(name="ps_w", bufs=2))
+
+        def load_list(name, src):
+            tile = lists.tile(list(src.shape), U16, name=name)
+            nc.sync.dma_start(tile[:], src)
+            return tile
+
+        d_byte_table = keep.tile([P, G], U8, name="d_byte_table")
+        x_byte_table = keep.tile([P, T], U8, name="x_byte_table")
+        nc.gpsimd.memset(d_byte_table[:].bitcast(I32), 0)
+        nc.gpsimd.memset(x_byte_table[:].bitcast(I32), 0)
+        nc.sync.dma_start(d_byte_table[0:P:8, :].bitcast(I32), d_scales[0].bitcast(I32))
+        nc.sync.dma_start(x_byte_table[0:P:8, :].bitcast(I32), x_scales[0].bitcast(I32))
+        ka_l = load_list("ka_l", ka)
+        kb_l = load_list("kb_l", kb)
+        offs_l = load_list("offs_l", offs)
+        n1_l = load_list("n1_l", n1)
+        n2_l = load_list("n2_l", n2)
+        d_word_table = keep.tile([P, G], U32, name="d_word_table")
+        nc.sync.dma_start(d_word_table[:].bitcast(I32), d_words[0].rearrange("p n t -> p (n t)").bitcast(I32))
+        x_word_table = keep.tile([P, T], U32, name="x_word_table", tag="late_w1")
+        nc.sync.dma_start(x_word_table[:].bitcast(I32), x_words[0].rearrange("p n t -> p (n t)").bitcast(I32))
+        n3_l = load_list("n3_l", n3)
+        n5_l = load_list("n5_l", n5)
+        n4_l = load_list("n4_l", n4)
+        gn_col = keep.tile([P, 4], F32, name="gn_col")
+        nc.gpsimd.dma_start(gn_col[:], gn.rearrange("(p t) o -> p (t o)", t=4))
+
+        ident = keep.tile([P, P], F32, name="ident")
+        make_identity(nc, ident[:])
+
+        pages = [keep.tile([P, U], F32, name="page%d" % m) for m in range(3)]
+        plane0 = keep.tile([P, 3 * PIECE], U8, name="plane0", align_bytes=64)
+        plane1 = keep.tile([P, 2 * PIECE], U8, name="plane1", tag="after_p", align_bytes=64)
+        nc.vector.memset(plane0[:].bitcast(I32), 0)
+        nc.vector.memset(plane1[:].bitcast(I32), 0)
+        nc.vector.memset(pages[0][:], 0.0)
+        nc.vector.memset(pages[1][:], 0.0)
+        nc.scalar.activation(pages[2][:], pages[0][:], COPY)
+
+        gn_ps = ps_w.tile([P, 4, P], F32, name="gn_ps", tag="w")
+        for t in range(4):
+            nc.tensor.transpose(gn_ps[:, t, :], gn_col[:, t : t + 1].to_broadcast([P, P]), ident[:])
+        gn_row = keep.tile([P, H], F32, name="gn_row")
+        nc.scalar.activation(gn_row[:].rearrange("q (n t) -> q n t", t=4), gn_ps[:].rearrange("q t n -> q n t"), COPY)
+
+        def place_scales(picked, plane, queue):
+            for q in range(4):
+                queue.dma_start(plane[32 * q : 32 * q + 4, :].bitcast(I32), picked[32 * q : 32 * q + 32 : 8, :].bitcast(I32))
+
+        def entries(lst, first, count):
+            return lst[:, first // 16 : (first + count) // 16]
+
+        bytes0 = keep.tile([P, 3 * PIECE], U8, name="bytes0")
+        nc.vector.tensor_copy(bytes0[:, 0:PIECE], d_byte_table[:].indirect(entries(ka_l, 0, PIECE)))
+        nc.vector.tensor_copy(bytes0[:, PIECE : 2 * PIECE], d_byte_table[:].indirect(entries(kb_l, 0, PIECE)))
+        nc.vector.tensor_copy(bytes0[:, 2 * PIECE :], x_byte_table[:].indirect(offs_l[:]))
+        place_scales(bytes0, plane0, nc.scalar)
+        ka_words0 = keep.tile([P, PIECE], U32, name="ka_words0", tag="after_a", align_bytes=64)
+        kb_words0 = keep.tile([P, PIECE], U32, name="kb_words0", tag="after_b", align_bytes=64)
+        x_picked = keep.tile([P, S], U32, name="x_picked", align_bytes=64)
+        nc.vector.tensor_copy(ka_words0[:], d_word_table[:].indirect(entries(ka_l, 0, PIECE)))
+        nc.vector.tensor_copy(kb_words0[:], d_word_table[:].indirect(entries(kb_l, 0, PIECE)))
+        nc.vector.tensor_copy(x_picked[:], x_word_table[:].indirect(offs_l[:]))
+        x_plane = plane0[:, 2 * PIECE :]
+
+        w_raw = keep.tile([P, 4, N], F32, name="w_raw", tag="late_w1")
+        nc.sync.dma_start(w_raw[:], w1.rearrange("(p j) n -> p j n", j=4))
+
+        h = [keep.tile([P, S], F32, name="h%d" % i) for i in range(4)]
+        pair = [keep.tile([P, 2, W], F32, name="pair%d" % i) for i in range(4)]
+        ranked = [keep.tile([P, 2, W], F32, name="ranked%d" % i, align_bytes=64) for i in range(4)]
+        dt = [keep.tile([P, S], F32, name="dt%d" % i, align_bytes=64) for i in range(4)]
+        neg = [[keep.tile([P, P], F32, name="neg%d_%d" % (i, c)) for c in range(2)] for i in range(4)]
+
+        def first_product(i, a_words, b_words, plane):
+            cols = slice((i % 2) * P, (i % 2 + 1) * P)
+            b_cols = slice(PIECE + cols.start, PIECE + cols.stop)
+            acc = ps_h.tile([P, S], F32, name="acc", tag="h") if i < 2 else ps_t.tile([P, S], F32, name="acc", tag="t")
+            nc.tensor.matmul_mx(acc[:], lhsT=a_words[:, cols].bitcast(FP8X4), lhsT_scale=plane[:, cols],
+                                rhs=x_picked[:].bitcast(FP8X4), rhs_scale=x_plane, start=True, stop=False)
+            nc.tensor.matmul_mx(acc[:], lhsT=b_words[:, cols].bitcast(FP8X4), lhsT_scale=plane[:, b_cols],
+                                rhs=x_picked[:].bitcast(FP8X4), rhs_scale=x_plane, start=False, stop=True)
+            nc.vector.tensor_scalar_mul(h[i][:], acc[:], 0.0625)
+
+        def fetch_pairs(i):
+            nc.scalar.activation(pair[i][:, 0, :], h[i][:].indirect(n1_l[:]), COPY)
+            nc.scalar.activation(pair[i][:, 1, :], h[i][:].indirect(n2_l[:]), COPY)
+            nc.vector.tensor_tensor(ranked[i][:, 0, :], pair[i][:, 0, :], pair[i][:, 1, :], ALU.max)
+            nc.vector.tensor_tensor(ranked[i][:, 1, :], pair[i][:, 0, :], pair[i][:, 1, :], ALU.min)
+
+        def put_back(i):
+            nc.scalar.activation(dt[i][:].indirect(n1_l[:]), ranked[i][:, 0, :], COPY)
+            nc.scalar.activation(dt[i][:].indirect(n2_l[:]), ranked[i][:, 1, :], COPY)
+
+        def difference(i, halves):
+            rows = slice(i * P, (i + 1) * P)
+            diff = ps_t.tile([P, len(halves), P], F32, name="diff", tag="t")
+            for k, c in enumerate(halves):
+                nc.scalar.activation(neg[i][c][:], dt[i][:].indirect(entries(n3_l, c * P, P)), COPY, scale=-1.0)
+                nc.tensor.matmul(diff[:, k, :], lhsT=dt[i][:, c * P : (c + 1) * P], rhs=ident[:], is_transpose=True, start=True, stop=False)
+                nc.tensor.matmul(diff[:, k, :], lhsT=neg[i][c][:], rhs=ident[:], is_transpose=True, start=False, stop=True)
+            nc.vector.tensor_tensor(z_t[:, halves[0] : halves[-1] + 1, rows], diff[:],
+                                    gn_row[:, rows].unsqueeze(1).to_broadcast([P, len(halves), P]), ALU.mult)
+
+        w_codes = keep.tile([P, N], U32, name="w_codes", align_bytes=64)
+        w_plane = keep.tile([P, N], U8, name="w_plane", align_bytes=64)
+
+        def quantise_w(cols):
+            nc.vector.tensor_copy(w_bf[:, cols, :].rearrange("p (c i) t -> p c t i", i=4),
+                                  w_raw[:, :, cols].rearrange("p t (c i) -> p c t i", i=4))
+            nc.vector.quantize_mx(w_codes[:, cols].bitcast(FP8X4), w_plane[:, cols],
+                                  w_bf[:, cols, :].rearrange("p n t -> p (n t)"))
+
+        first_product(0, ka_words0, kb_words0, plane0)
+        first_product(1, ka_words0, kb_words0, plane0)
+        fetch_pairs(0)
+
+        bytes1 = keep.tile([P, 2 * PIECE], U8, name="bytes1", tag="after_a", align_bytes=64)
+        nc.vector.tensor_copy(bytes1[:, 0:PIECE], d_byte_table[:].indirect(entries(ka_l, PIECE, PIECE)))
+        nc.vector.tensor_copy(bytes1[:, PIECE:], d_byte_table[:].indirect(entries(kb_l, PIECE, PIECE)))
+        place_scales(bytes1, plane1, nc.sync)
+        fetch_pairs(1)
+        put_back(0)
+        words1 = keep.tile([P, 2, PIECE], U32, name="words1", tag="after_b", align_bytes=64)
+        nc.vector.tensor_copy(words1[:, 0, :], d_word_table[:].indirect(entries(ka_l, PIECE, PIECE)))
+        nc.vector.tensor_copy(words1[:, 1, :], d_word_table[:].indirect(entries(kb_l, PIECE, PIECE)))
+        first_product(2, words1[:, 0, :], words1[:, 1, :], plane1)
+        first_product(3, words1[:, 0, :], words1[:, 1, :], plane1)
+        z_t = keep.tile([P, 2, H], BF16, name="z_t", tag="after_b", align_bytes=64)
+        w_bf = keep.tile([P, N, 4], BF16, name="w_bf", tag="after_p", align_bytes=64)
+        put_back(1)
+        fetch_pairs(2)
+        fetch_pairs(3)
+        quantise_w(slice(0, N // 2))
+        quantise_w(slice(N // 2, N))
+        difference(0, [0, 1])
+        difference(1, [0, 1])
+        put_back(2)
+        put_back(3)
+        difference(2, [0, 1])
+        difference(3, [0])
+        difference(3, [1])
+
+        z_bf = [keep.tile([P, P, 4], BF16, name="z_bf%d" % c, align_bytes=64) for c in range(2)]
+        z_codes = [keep.tile([P, P], U32, name="z_codes%d" % c, align_bytes=64) for c in range(2)]
+        z_plane = [keep.tile([P, P], U8, name="z_plane%d" % c, align_bytes=64) for c in range(2)]
+
+        def quantise_z(c):
+            words = z_t[:, c, :].bitcast(F32)
+            turned = ps_w.tile([P, 2, P], F32, name="turned", tag="w")
+            for u in range(2):
+                nc.tensor.transpose(turned[:, u, :], words[:, u : 2 * P : 2], ident[:])
+            nc.vector.tensor_copy(z_bf[c][:].rearrange("p j t -> p (j t)").bitcast(F32).rearrange("p (j u) -> p j u", u=2),
+                                  turned[:].rearrange("p u j -> p j u"))
+            nc.vector.quantize_mx(z_codes[c][:].bitcast(FP8X4), z_plane[c][:], z_bf[c][:].rearrange("p j t -> p (j t)"))
+
+        h2 = [keep.tile([P, S], F32, name="h2_%d" % m) for m in range(4)]
+        acc2 = [None] + [ps_h.tile([P, S], F32, name="acc2_%d" % m, tag="h") for m in range(1, 4)]
+
+        def second_product(c):
+            half = slice(c * P, (c + 1) * P)
+            for m in range(4):
+                cols = slice(m * P, (m + 1) * P)
+                if m == 0:
+                    first = ps_t.tile([P, P], F32, name="first", tag="t")
+                nc.tensor.matmul_mx(first[:] if m == 0 else acc2[m][:, half], lhsT=w_codes[:, cols].bitcast(FP8X4), lhsT_scale=w_plane[:, cols],
+                                    rhs=z_codes[c][:].bitcast(FP8X4), rhs_scale=z_plane[c][:], start=True, stop=True)
+            nc.scalar.activation(h2[0][:, half], first[:], COPY)
+
+        quantise_z(0)
+        quantise_z(1)
+        second_product(0)
+        second_product(1)
+        for m in range(1, 4):
+            nc.vector.tensor_copy(h2[m][:], acc2[m][:])
+
+        other = [keep.tile([P, S], F32, name="other%d" % m) for m in range(4)]
+        nw = [keep.tile([P, S], F32, name="nw%d" % m) for m in range(4)]
+
+        def larger(m):
+            for c in range(2):
+                nc.scalar.activation(other[m][:, c * P : (c + 1) * P], h2[m][:].indirect(entries(n5_l, c * P, P)), COPY)
+            nc.vector.tensor_tensor(nw[m][:], h2[m][:], other[m][:], ALU.max)
+
+        def put_out(m):
+            nc.scalar.activation(pages[m % 3][:].indirect(n4_l[:]), nw[m][:], COPY)
+            nc.sync.dma_start(out[m * P : (m + 1) * P, :], pages[m % 3][:])
+
+        larger(0)
+        for m in range(4):
+            if m + 1 < 4:
+                larger(m + 1)
+            put_out(m)

@@ -18,6 +18,7 @@ COPY = mybir.ActivationFunctionType.Copy
 
 P = 128
 PIECE = 256
+WIDE = S + 16
 
 
 def tile_picked_aqlorddpags_none_p_kernel(
@@ -38,17 +39,19 @@ def tile_picked_aqlorddpags_none_p_kernel(
 
         d_byte_table = keep.tile([P, G], U8, name="d_byte_table")
         x_byte_table = keep.tile([P, T], U8, name="x_byte_table")
-        nc.gpsimd.memset(d_byte_table[:].bitcast(I32), 0)
-        nc.gpsimd.memset(x_byte_table[:].bitcast(I32), 0)
-        nc.sync.dma_start(d_byte_table[0:P:8, :].bitcast(I32), d_scales[0].bitcast(I32))
-        nc.sync.dma_start(x_byte_table[0:P:8, :].bitcast(I32), x_scales[0].bitcast(I32))
+        def load_scale_rows(table, rows):
+            words = rows.bitcast(I32)
+            nc.sync.dma_start(table[:].bitcast(I32), words.unsqueeze(1).to_broadcast([16, 8, words.shape[1]]))
+
+        load_scale_rows(d_byte_table, d_scales[0])
         ka_l = load_list("ka_l", ka)
         kb_l = load_list("kb_l", kb)
+        load_scale_rows(x_byte_table, x_scales[0])
         offs_l = load_list("offs_l", offs)
-        n1_l = load_list("n1_l", n1)
-        n2_l = load_list("n2_l", n2)
         d_word_table = keep.tile([P, G], U32, name="d_word_table")
         nc.sync.dma_start(d_word_table[:].bitcast(I32), d_words[0].rearrange("p n t -> p (n t)").bitcast(I32))
+        n1_l = load_list("n1_l", n1)
+        n2_l = load_list("n2_l", n2)
         x_word_table = keep.tile([P, T], U32, name="x_word_table", tag="late_w1")
         nc.sync.dma_start(x_word_table[:].bitcast(I32), x_words[0].rearrange("p n t -> p (n t)").bitcast(I32))
         n3_l = load_list("n3_l", n3)
@@ -72,8 +75,6 @@ def tile_picked_aqlorddpags_none_p_kernel(
         gn_ps = ps_w.tile([P, 4, P], F32, name="gn_ps", tag="w")
         for t in range(4):
             nc.tensor.transpose(gn_ps[:, t, :], gn_col[:, t : t + 1].to_broadcast([P, P]), ident[:])
-        gn_row = keep.tile([P, H], F32, name="gn_row")
-        nc.scalar.activation(gn_row[:].rearrange("q (n t) -> q n t", t=4), gn_ps[:].rearrange("q t n -> q n t"), COPY)
 
         def place_scales(picked, plane, queue):
             for q in range(4):
@@ -82,11 +83,13 @@ def tile_picked_aqlorddpags_none_p_kernel(
         def entries(lst, first, count):
             return lst[:, first // 16 : (first + count) // 16]
 
-        bytes0 = keep.tile([P, 3 * PIECE], U8, name="bytes0")
+        bytes0 = keep.tile([P, 3 * PIECE], U8, name="bytes0", tag="after_moves")
         nc.vector.tensor_copy(bytes0[:, 0:PIECE], d_byte_table[:].indirect(entries(ka_l, 0, PIECE)))
         nc.vector.tensor_copy(bytes0[:, PIECE : 2 * PIECE], d_byte_table[:].indirect(entries(kb_l, 0, PIECE)))
         nc.vector.tensor_copy(bytes0[:, 2 * PIECE :], x_byte_table[:].indirect(offs_l[:]))
         place_scales(bytes0, plane0, nc.scalar)
+        gn_row = keep.tile([P, H], F32, name="gn_row", tag="after_moves")
+        nc.scalar.activation(gn_row[:].rearrange("q (n t) -> q n t", t=4), gn_ps[:].rearrange("q t n -> q n t"), COPY)
         ka_words0 = keep.tile([P, PIECE], U32, name="ka_words0", tag="after_a", align_bytes=64)
         kb_words0 = keep.tile([P, PIECE], U32, name="kb_words0", tag="after_b", align_bytes=64)
         x_picked = keep.tile([P, S], U32, name="x_picked", align_bytes=64)
@@ -101,8 +104,10 @@ def tile_picked_aqlorddpags_none_p_kernel(
         h = [keep.tile([P, S], F32, name="h%d" % i) for i in range(4)]
         pair = [keep.tile([P, 2, W], F32, name="pair%d" % i) for i in range(4)]
         ranked = [keep.tile([P, 2, W], F32, name="ranked%d" % i, align_bytes=64) for i in range(4)]
-        dt = [keep.tile([P, S], F32, name="dt%d" % i, align_bytes=64) for i in range(4)]
-        neg = [[keep.tile([P, P], F32, name="neg%d_%d" % (i, c)) for c in range(2)] for i in range(4)]
+        dt = [keep.tile([P, WIDE if i < 2 else S], F32, name="dt%d" % i, align_bytes=64) for i in range(4)]
+        h2 = [keep.tile([P, WIDE], F32, name="h2_%d" % m) for m in range(4)]
+        for wide in dt[:2] + h2:
+            nc.gpsimd.memset(wide[:, S:], 0.0)
 
         def first_product(i, a_words, b_words, plane):
             cols = slice((i % 2) * P, (i % 2 + 1) * P)
@@ -120,19 +125,22 @@ def tile_picked_aqlorddpags_none_p_kernel(
             nc.vector.tensor_tensor(ranked[i][:, 0, :], pair[i][:, 0, :], pair[i][:, 1, :], ALU.max)
             nc.vector.tensor_tensor(ranked[i][:, 1, :], pair[i][:, 0, :], pair[i][:, 1, :], ALU.min)
 
-        def put_back(i):
-            nc.scalar.activation(dt[i][:].indirect(n1_l[:]), ranked[i][:, 0, :], COPY)
-            nc.scalar.activation(dt[i][:].indirect(n2_l[:]), ranked[i][:, 1, :], COPY)
+        def put_back(tiles):
+            for k, lst in enumerate((n1_l, n2_l)):
+                for i in tiles:
+                    nc.scalar.activation(dt[i][:].indirect(lst[:]), ranked[i][:, k, :], COPY)
 
-        def difference(i, halves):
+        def difference(i, first, count, tag):
             rows = slice(i * P, (i + 1) * P)
-            diff = ps_t.tile([P, len(halves), P], F32, name="diff", tag="t")
-            for k, c in enumerate(halves):
-                nc.scalar.activation(neg[i][c][:], dt[i][:].indirect(entries(n3_l, c * P, P)), COPY, scale=-1.0)
+            neg = keep.tile([P, count * P], F32, name="neg", tag=tag, align_bytes=64)
+            nc.scalar.activation(neg[:], dt[i][:].indirect(entries(n3_l, first * P, count * P)), COPY, scale=-1.0)
+            diff = ps_t.tile([P, count, P], F32, name="diff", tag="t")
+            for k in range(count):
+                c = first + k
                 nc.tensor.matmul(diff[:, k, :], lhsT=dt[i][:, c * P : (c + 1) * P], rhs=ident[:], is_transpose=True, start=True, stop=False)
-                nc.tensor.matmul(diff[:, k, :], lhsT=neg[i][c][:], rhs=ident[:], is_transpose=True, start=False, stop=True)
-            nc.vector.tensor_tensor(z_t[:, halves[0] : halves[-1] + 1, rows], diff[:],
-                                    gn_row[:, rows].unsqueeze(1).to_broadcast([P, len(halves), P]), ALU.mult)
+                nc.tensor.matmul(diff[:, k, :], lhsT=neg[:, k * P : (k + 1) * P], rhs=ident[:], is_transpose=True, start=False, stop=True)
+            nc.vector.tensor_tensor(z_t[:, first : first + count, rows], diff[:],
+                                    gn_row[:, rows].unsqueeze(1).to_broadcast([P, count, P]), ALU.mult)
 
         w_codes = keep.tile([P, N], U32, name="w_codes", align_bytes=64)
         w_plane = keep.tile([P, N], U8, name="w_plane", align_bytes=64)
@@ -152,7 +160,7 @@ def tile_picked_aqlorddpags_none_p_kernel(
         nc.vector.tensor_copy(bytes1[:, PIECE:], d_byte_table[:].indirect(entries(kb_l, PIECE, PIECE)))
         place_scales(bytes1, plane1, nc.sync)
         fetch_pairs(1)
-        put_back(0)
+        put_back((0, 1))
         words1 = keep.tile([P, 2, PIECE], U32, name="words1", tag="after_b", align_bytes=64)
         nc.vector.tensor_copy(words1[:, 0, :], d_word_table[:].indirect(entries(ka_l, PIECE, PIECE)))
         nc.vector.tensor_copy(words1[:, 1, :], d_word_table[:].indirect(entries(kb_l, PIECE, PIECE)))
@@ -160,59 +168,52 @@ def tile_picked_aqlorddpags_none_p_kernel(
         first_product(3, words1[:, 0, :], words1[:, 1, :], plane1)
         z_t = keep.tile([P, 2, H], BF16, name="z_t", tag="after_b", align_bytes=64)
         w_bf = keep.tile([P, N, 4], BF16, name="w_bf", tag="after_p", align_bytes=64)
-        put_back(1)
         fetch_pairs(2)
         fetch_pairs(3)
         quantise_w(slice(0, N // 2))
         quantise_w(slice(N // 2, N))
-        difference(0, [0, 1])
-        difference(1, [0, 1])
-        put_back(2)
-        put_back(3)
-        difference(2, [0, 1])
-        difference(3, [0])
-        difference(3, [1])
+        difference(0, 0, 2, "neg0")
+        difference(1, 0, 2, "neg1")
+        put_back((2, 3))
+        difference(2, 0, 1, "neg2")
+        difference(3, 0, 1, "neg3")
+        difference(2, 1, 1, "ranked3")
+        difference(3, 1, 1, "neg4")
 
         z_bf = [keep.tile([P, P, 4], BF16, name="z_bf%d" % c, align_bytes=64) for c in range(2)]
-        z_codes = [keep.tile([P, P], U32, name="z_codes%d" % c, align_bytes=64) for c in range(2)]
-        z_plane = [keep.tile([P, P], U8, name="z_plane%d" % c, align_bytes=64) for c in range(2)]
+        z_codes = keep.tile([P, S], U32, name="z_codes", align_bytes=64)
+        z_plane = keep.tile([P, S], U8, name="z_plane", align_bytes=64)
 
-        def quantise_z(c):
+        def quantise_z(c, copy):
+            half = slice(c * P, (c + 1) * P)
             words = z_t[:, c, :].bitcast(F32)
             turned = ps_w.tile([P, 2, P], F32, name="turned", tag="w")
             for u in range(2):
                 nc.tensor.transpose(turned[:, u, :], words[:, u : 2 * P : 2], ident[:])
-            nc.vector.tensor_copy(z_bf[c][:].rearrange("p j t -> p (j t)").bitcast(F32).rearrange("p (j u) -> p j u", u=2),
-                                  turned[:].rearrange("p u j -> p j u"))
-            nc.vector.quantize_mx(z_codes[c][:].bitcast(FP8X4), z_plane[c][:], z_bf[c][:].rearrange("p j t -> p (j t)"))
+            copy(z_bf[c][:].rearrange("p j t -> p (j t)").bitcast(F32).rearrange("p (j u) -> p j u", u=2),
+                 turned[:].rearrange("p u j -> p j u"))
+            nc.vector.quantize_mx(z_codes[:, half].bitcast(FP8X4), z_plane[:, half], z_bf[c][:].rearrange("p j t -> p (j t)"))
 
-        h2 = [keep.tile([P, S], F32, name="h2_%d" % m) for m in range(4)]
-        acc2 = [None] + [ps_h.tile([P, S], F32, name="acc2_%d" % m, tag="h") for m in range(1, 4)]
+        def second_product(m, cols, copy):
+            rows = slice(m * P, (m + 1) * P)
+            acc = ps_h.tile([P, cols.stop - cols.start], F32, name="acc", tag="h")
+            nc.tensor.matmul_mx(acc[:], lhsT=w_codes[:, rows].bitcast(FP8X4), lhsT_scale=w_plane[:, rows],
+                                rhs=z_codes[:, cols].bitcast(FP8X4), rhs_scale=z_plane[:, cols], start=True, stop=True)
+            copy(h2[m][:, cols], acc[:])
 
-        def second_product(c):
-            half = slice(c * P, (c + 1) * P)
-            for m in range(4):
-                cols = slice(m * P, (m + 1) * P)
-                if m == 0:
-                    first = ps_t.tile([P, P], F32, name="first", tag="t")
-                nc.tensor.matmul_mx(first[:] if m == 0 else acc2[m][:, half], lhsT=w_codes[:, cols].bitcast(FP8X4), lhsT_scale=w_plane[:, cols],
-                                    rhs=z_codes[c][:].bitcast(FP8X4), rhs_scale=z_plane[c][:], start=True, stop=True)
-            nc.scalar.activation(h2[0][:, half], first[:], COPY)
-
-        quantise_z(0)
-        quantise_z(1)
-        second_product(0)
-        second_product(1)
+        quantise_z(0, nc.scalar.copy)
+        quantise_z(1, nc.scalar.copy)
+        second_product(0, slice(0, P), nc.scalar.copy)
+        second_product(0, slice(P, S), nc.vector.tensor_copy)
         for m in range(1, 4):
-            nc.vector.tensor_copy(h2[m][:], acc2[m][:])
+            second_product(m, slice(0, S), nc.vector.tensor_copy)
 
         other = [keep.tile([P, S], F32, name="other%d" % m) for m in range(4)]
         nw = [keep.tile([P, S], F32, name="nw%d" % m) for m in range(4)]
 
         def larger(m):
-            for c in range(2):
-                nc.scalar.activation(other[m][:, c * P : (c + 1) * P], h2[m][:].indirect(entries(n5_l, c * P, P)), COPY)
-            nc.vector.tensor_tensor(nw[m][:], h2[m][:], other[m][:], ALU.max)
+            nc.scalar.activation(other[m][:], h2[m][:].indirect(n5_l[:]), COPY)
+            nc.vector.tensor_tensor(nw[m][:], h2[m][:, :S], other[m][:], ALU.max)
 
         def put_out(m):
             nc.scalar.activation(pages[m % 3][:].indirect(n4_l[:]), nw[m][:], COPY)

from contextlib import ExitStack

import concourse.mybir as mybir
from concourse.masks import make_identity

K, T, S, N, G, H, W, U = 512, 1024, 256, 512, 2048, 512, 128, 1024
FLOPS = 2 * (2 * K * H * S) + 2 * H * N * S

F32 = mybir.dt.float32
BF16 = mybir.dt.bfloat16
I32 = mybir.dt.int32
U32 = mybir.dt.uint32
U16 = mybir.dt.uint16
U8 = mybir.dt.uint8
FP8X4 = mybir.dt.float8_e4m3fn_x4
ALU = mybir.AluOpType
COPY = mybir.ActivationFunctionType.Copy

P = 128
PIECE = 256
WIDE = S + 16


def tile_picked_aqlorddpags_none_p_kernel(
    tc, x_words, x_scales, d_words, d_scales, gn, w1, offs, ka, kb, n1, n2, n3, n4, n5, out
):
    nc = tc.nc
    with ExitStack() as ctx:
        lists = ctx.enter_context(tc.tile_pool(name="lists", bufs=1))
        keep = ctx.enter_context(tc.tile_pool(name="keep", bufs=1))
        ps_h = ctx.enter_context(tc.psum_pool(name="ps_h", bufs=4))
        ps_t = ctx.enter_context(tc.psum_pool(name="ps_t", bufs=2))
        ps_w = ctx.enter_context(tc.psum_pool(name="ps_w", bufs=2))

        def load_list(name, src):
            tile = lists.tile(list(src.shape), U16, name=name)
            nc.sync.dma_start(tile[:], src)
            return tile

        d_byte_table = keep.tile([P, G], U8, name="d_byte_table")
        x_byte_table = keep.tile([P, T], U8, name="x_byte_table")
        def load_scale_rows(table, rows):
            words = rows.bitcast(I32)
            nc.sync.dma_start(table[:].bitcast(I32), words.unsqueeze(1).to_broadcast([16, 8, words.shape[1]]))

        load_scale_rows(d_byte_table, d_scales[0])
        ka_l = load_list("ka_l", ka)
        kb_l = load_list("kb_l", kb)
        load_scale_rows(x_byte_table, x_scales[0])
        offs_l = load_list("offs_l", offs)
        d_word_table = keep.tile([P, G], U32, name="d_word_table")
        nc.sync.dma_start(d_word_table[:].bitcast(I32), d_words[0].rearrange("p n t -> p (n t)").bitcast(I32))
        n1_l = load_list("n1_l", n1)
        n2_l = load_list("n2_l", n2)
        x_word_table = keep.tile([P, T], U32, name="x_word_table", tag="late_w1")
        nc.sync.dma_start(x_word_table[:].bitcast(I32), x_words[0].rearrange("p n t -> p (n t)").bitcast(I32))
        n3_l = load_list("n3_l", n3)
        n5_l = load_list("n5_l", n5)
        n4_l = load_list("n4_l", n4)
        gn_col = keep.tile([P, 4], F32, name="gn_col")
        nc.gpsimd.dma_start(gn_col[:], gn.rearrange("(p t) o -> p (t o)", t=4))

        ident = keep.tile([P, P], F32, name="ident")
        make_identity(nc, ident[:])

        pages = [keep.tile([P, U], F32, name="page%d" % m) for m in range(3)]
        plane0 = keep.tile([P, 3 * PIECE], U8, name="plane0", align_bytes=64)
        plane1 = keep.tile([P, 2 * PIECE], U8, name="plane1", tag="after_p", align_bytes=64)
        nc.vector.memset(plane0[:].bitcast(I32), 0)
        nc.vector.memset(plane1[:].bitcast(I32), 0)
        nc.vector.memset(pages[0][:], 0.0)
        nc.vector.memset(pages[1][:], 0.0)
        nc.scalar.activation(pages[2][:], pages[0][:], COPY)

        gn_ps = ps_w.tile([P, 4, P], F32, name="gn_ps", tag="w")
        for t in range(4):
            nc.tensor.transpose(gn_ps[:, t, :], gn_col[:, t : t + 1].to_broadcast([P, P]), ident[:])

        def place_scales(picked, plane, queue):
            for q in range(4):
                queue.dma_start(plane[32 * q : 32 * q + 4, :].bitcast(I32), picked[32 * q : 32 * q + 32 : 8, :].bitcast(I32))

        def entries(lst, first, count):
            return lst[:, first // 16 : (first + count) // 16]

        bytes0 = keep.tile([P, 3 * PIECE], U8, name="bytes0", tag="after_moves")
        nc.vector.tensor_copy(bytes0[:, 0:PIECE], d_byte_table[:].indirect(entries(ka_l, 0, PIECE)))
        nc.vector.tensor_copy(bytes0[:, PIECE : 2 * PIECE], d_byte_table[:].indirect(entries(kb_l, 0, PIECE)))
        nc.vector.tensor_copy(bytes0[:, 2 * PIECE :], x_byte_table[:].indirect(offs_l[:]))
        place_scales(bytes0, plane0, nc.scalar)
        gn_row = keep.tile([P, H], F32, name="gn_row", tag="after_moves")
        nc.scalar.activation(gn_row[:].rearrange("q (n t) -> q n t", t=4), gn_ps[:].rearrange("q t n -> q n t"), COPY)
        ka_words0 = keep.tile([P, PIECE], U32, name="ka_words0", tag="after_a", align_bytes=64)
        kb_words0 = keep.tile([P, PIECE], U32, name="kb_words0", tag="after_b", align_bytes=64)
        x_picked = keep.tile([P, S], U32, name="x_picked", align_bytes=64)
        nc.vector.tensor_copy(ka_words0[:], d_word_table[:].indirect(entries(ka_l, 0, PIECE)))
        nc.vector.tensor_copy(kb_words0[:], d_word_table[:].indirect(entries(kb_l, 0, PIECE)))
        nc.vector.tensor_copy(x_picked[:], x_word_table[:].indirect(offs_l[:]))
        x_plane = plane0[:, 2 * PIECE :]

        w_raw = keep.tile([P, 4, N], F32, name="w_raw", tag="late_w1")
        nc.sync.dma_start(w_raw[:], w1.rearrange("(p j) n -> p j n", j=4))

        h = [keep.tile([P, S], F32, name="h%d" % i) for i in range(4)]
        pair = [keep.tile([P, 2, W], F32, name="pair%d" % i) for i in range(4)]
        ranked = [keep.tile([P, 2, W], F32, name="ranked%d" % i, align_bytes=64) for i in range(4)]
        dt = [keep.tile([P, WIDE if i < 2 else S], F32, name="dt%d" % i, align_bytes=64) for i in range(4)]
        h2 = [keep.tile([P, WIDE], F32, name="h2_%d" % m) for m in range(4)]
        for wide in dt[:2] + h2:
            nc.gpsimd.memset(wide[:, S:], 0.0)

        def first_product(i, a_words, b_words, plane):
            cols = slice((i % 2) * P, (i % 2 + 1) * P)
            b_cols = slice(PIECE + cols.start, PIECE + cols.stop)
            acc = ps_h.tile([P, S], F32, name="acc", tag="h") if i < 2 else ps_t.tile([P, S], F32, name="acc", tag="t")
            nc.tensor.matmul_mx(acc[:], lhsT=a_words[:, cols].bitcast(FP8X4), lhsT_scale=plane[:, cols],
                                rhs=x_picked[:].bitcast(FP8X4), rhs_scale=x_plane, start=True, stop=False)
            nc.tensor.matmul_mx(acc[:], lhsT=b_words[:, cols].bitcast(FP8X4), lhsT_scale=plane[:, b_cols],
                                rhs=x_picked[:].bitcast(FP8X4), rhs_scale=x_plane, start=False, stop=True)
            nc.vector.tensor_scalar_mul(h[i][:], acc[:], 0.0625)

        def fetch_pairs(i):
            nc.scalar.activation(pair[i][:, 0, :], h[i][:].indirect(n1_l[:]), COPY)
            nc.scalar.activation(pair[i][:, 1, :], h[i][:].indirect(n2_l[:]), COPY)
            nc.vector.tensor_tensor(ranked[i][:, 0, :], pair[i][:, 0, :], pair[i][:, 1, :], ALU.max)
            nc.vector.tensor_tensor(ranked[i][:, 1, :], pair[i][:, 0, :], pair[i][:, 1, :], ALU.min)

        def put_back(tiles):
            for k, lst in enumerate((n1_l, n2_l)):
                for i in tiles:
                    nc.scalar.activation(dt[i][:].indirect(lst[:]), ranked[i][:, k, :], COPY)

        def difference(i, first, count, tag):
            rows = slice(i * P, (i + 1) * P)
            neg = keep.tile([P, count * P], F32, name="neg", tag=tag, align_bytes=64)
            nc.scalar.activation(neg[:], dt[i][:].indirect(entries(n3_l, first * P, count * P)), COPY, scale=-1.0)
            diff = ps_t.tile([P, count, P], F32, name="diff", tag="t")
            for k in range(count):
                c = first + k
                nc.tensor.matmul(diff[:, k, :], lhsT=dt[i][:, c * P : (c + 1) * P], rhs=ident[:], is_transpose=True, start=True, stop=False)
                nc.tensor.matmul(diff[:, k, :], lhsT=neg[:, k * P : (k + 1) * P], rhs=ident[:], is_transpose=True, start=False, stop=True)
            nc.vector.tensor_tensor(z_t[:, first : first + count, rows], diff[:],
                                    gn_row[:, rows].unsqueeze(1).to_broadcast([P, count, P]), ALU.mult)

        w_codes = keep.tile([P, N], U32, name="w_codes", align_bytes=64)
        w_plane = keep.tile([P, N], U8, name="w_plane", align_bytes=64)

        def quantise_w(cols):
            nc.vector.tensor_copy(w_bf[:, cols, :].rearrange("p (c i) t -> p c t i", i=4),
                                  w_raw[:, :, cols].rearrange("p t (c i) -> p c t i", i=4))
            nc.vector.quantize_mx(w_codes[:, cols].bitcast(FP8X4), w_plane[:, cols],
                                  w_bf[:, cols, :].rearrange("p n t -> p (n t)"))

        first_product(0, ka_words0, kb_words0, plane0)
        first_product(1, ka_words0, kb_words0, plane0)
        fetch_pairs(0)

        bytes1 = keep.tile([P, 2 * PIECE], U8, name="bytes1", tag="after_a", align_bytes=64)
        nc.vector.tensor_copy(bytes1[:, 0:PIECE], d_byte_table[:].indirect(entries(ka_l, PIECE, PIECE)))
        nc.vector.tensor_copy(bytes1[:, PIECE:], d_byte_table[:].indirect(entries(kb_l, PIECE, PIECE)))
        place_scales(bytes1, plane1, nc.sync)
        fetch_pairs(1)
        put_back((0, 1))
        words1 = keep.tile([P, 2, PIECE], U32, name="words1", tag="after_b", align_bytes=64)
        nc.vector.tensor_copy(words1[:, 0, :], d_word_table[:].indirect(entries(ka_l, PIECE, PIECE)))
        nc.vector.tensor_copy(words1[:, 1, :], d_word_table[:].indirect(entries(kb_l, PIECE, PIECE)))
        first_product(2, words1[:, 0, :], words1[:, 1, :], plane1)
        first_product(3, words1[:, 0, :], words1[:, 1, :], plane1)
        z_t = keep.tile([P, 2, H], BF16, name="z_t", tag="after_b", align_bytes=64)
        w_bf = keep.tile([P, N, 4], BF16, name="w_bf", tag="after_p", align_bytes=64)
        fetch_pairs(2)
        fetch_pairs(3)
        quantise_w(slice(0, N // 2))
        quantise_w(slice(N // 2, N))
        difference(0, 0, 2, "neg0")
        difference(1, 0, 2, "neg1")
        put_back((2, 3))
        difference(2, 0, 1, "neg2")
        difference(3, 0, 1, "neg3")
        difference(2, 1, 1, "ranked3")
        difference(3, 1, 1, "neg4")

        z_bf = [keep.tile([P, P, 4], BF16, name="z_bf%d" % c, align_bytes=64) for c in range(2)]
        z_codes = keep.tile([P, S], U32, name="z_codes", align_bytes=64)
        z_plane = keep.tile([P, S], U8, name="z_plane", align_bytes=64)

        def quantise_z(c, copy):
            half = slice(c * P, (c + 1) * P)
            words = z_t[:, c, :].bitcast(F32)
            turned = ps_w.tile([P, 2, P], F32, name="turned", tag="w")
            for u in range(2):
                nc.tensor.transpose(turned[:, u, :], words[:, u : 2 * P : 2], ident[:])
            copy(z_bf[c][:].rearrange("p j t -> p (j t)").bitcast(F32).rearrange("p (j u) -> p j u", u=2),
                 turned[:].rearrange("p u j -> p j u"))
            nc.vector.quantize_mx(z_codes[:, half].bitcast(FP8X4), z_plane[:, half], z_bf[c][:].rearrange("p j t -> p (j t)"))

        def second_product(m, cols, copy):
            rows = slice(m * P, (m + 1) * P)
            acc = ps_h.tile([P, cols.stop - cols.start], F32, name="acc", tag="h")
            nc.tensor.matmul_mx(acc[:], lhsT=w_codes[:, rows].bitcast(FP8X4), lhsT_scale=w_plane[:, rows],
                                rhs=z_codes[:, cols].bitcast(FP8X4), rhs_scale=z_plane[:, cols], start=True, stop=True)
            copy(h2[m][:, cols], acc[:])

        quantise_z(0, nc.scalar.copy)
        quantise_z(1, nc.scalar.copy)
        second_product(0, slice(0, P), nc.scalar.copy)
        second_product(0, slice(P, S), nc.vector.tensor_copy)
        for m in range(1, 4):
            second_product(m, slice(0, S), nc.vector.tensor_copy)

        other = [keep.tile([P, S], F32, name="other%d" % m) for m in range(4)]
        nw = [keep.tile([P, S], F32, name="nw%d" % m) for m in range(4)]

        def larger(m):
            nc.scalar.activation(other[m][:], h2[m][:].indirect(n5_l[:]), COPY)
            nc.vector.tensor_tensor(nw[m][:], h2[m][:, :S], other[m][:], ALU.max)

        def put_out(m):
            nc.scalar.activation(pages[m % 3][:].indirect(n4_l[:]), nw[m][:], COPY)
            nc.sync.dma_start(out[m * P : (m + 1) * P, :], pages[m % 3][:])

        larger(0)
        for m in range(4):
            if m + 1 < 4:
                larger(m + 1)
            put_out(m)
